import numpy as np
import ml_dtypes


def mxq(x, axis, fmt="e4m3"):
    dtype, down = {"e4m3": (ml_dtypes.float8_e4m3fn, 7), "e5m2": (ml_dtypes.float8_e5m2, 14)}[fmt]
    v = np.moveaxis(np.asarray(x, np.float32).astype(ml_dtypes.bfloat16).astype(np.float64), axis, -1)
    blocks = v.reshape(v.shape[:-1] + (-1, 32))
    amax = np.abs(blocks).max(-1, keepdims=True)
    byte = np.maximum(np.where(amax > 0, np.frexp(amax)[1] - 1 + 127, 0) - down, 1)
    scale = np.exp2(byte - 127.0)
    codes = (blocks / scale).astype(np.float32).astype(dtype).astype(np.float64)
    return np.moveaxis((codes * scale).reshape(v.shape), -1, axis)


WIDE = False


def mx_kscale(k):
    if not WIDE:
        return np.ones(k)
    levels = np.array([10, -10, 5, -5, 0])
    if k % 512:
        return np.exp2(np.random.permutation(np.resize(levels, k // 32))).repeat(32)
    a = np.empty((k // 512, 16))
    for p in range(k // 512):
        a[p, :8] = np.random.permutation(np.resize(levels, 8))
        for g in range(8):
            far = levels[np.abs(levels - a[p, g]) >= 10]
            a[p, g + 8] = far[np.random.randint(len(far))]
    return np.exp2(a.ravel()).repeat(32)


def f64(x):
    return np.asarray(x).astype(np.float64)


def striped(idx):
    return np.tile(idx.reshape(-1, 16).T, (8, 1)).astype(np.uint16)


def unstriped(offs):
    return offs[:16].T.reshape(-1).astype(np.int64)


E2M1 = np.array([0.0, 0.5, 1.0, 1.5, 2.0, 3.0, 4.0, 6.0, -0.0, -0.5, -1.0, -1.5, -2.0, -3.0, -4.0, -6.0])


def pack_weight(w, fmt):
    k, n = w.shape
    w = f64(np.asarray(w, np.float32).astype(ml_dtypes.bfloat16)).reshape(k // 32, 32, n)
    amax = np.abs(w).max(1)
    if fmt == "e4m3":
        byte = np.frexp(amax)[1] - 1 + 127 - 7
    else:
        mant, ex = np.frexp(amax / 6.0)
        byte = np.where(mant > 0.5, ex, ex - 1) + 127
    byte = np.clip(np.where(amax > 0, byte, 1), 1, 254)
    scaled = (w * np.exp2(127.0 - byte)[:, None, :]).reshape(k, n).astype(np.float32)
    by_word = np.ascontiguousarray(scaled.reshape(k // 512, 128, 4, n).transpose(0, 1, 3, 2))
    if fmt == "e4m3":
        words = by_word.astype(ml_dtypes.float8_e4m3fn).view(np.uint8)
    else:
        c = by_word.astype(ml_dtypes.float4_e2m1fn).view(np.uint8) & 0xF
        words = (c[..., 0::2] | (c[..., 1::2] << 4)).reshape(k // 512, 128, 2 * n)
    return np.ascontiguousarray(words), np.ascontiguousarray(byte.astype(np.uint8).reshape(k // 512, 16, n))


def unpack_weight(words, scales, fmt):
    g, _, n = scales.shape
    words = np.ascontiguousarray(words).reshape(g, 128, n, -1)
    if fmt == "e4m3":
        vals = words.view(ml_dtypes.float8_e4m3fn).astype(np.float64)
    else:
        nib = np.empty((g, 128, n, 4), np.uint8)
        nib[..., 0::2] = words & 0xF
        nib[..., 1::2] = words >> 4
        vals = E2M1[nib]
    vals = vals * np.repeat(np.exp2(scales.astype(np.float64) - 127.0), 8, axis=1)[..., None]
    return vals.transpose(0, 1, 3, 2).reshape(g * 512, n)


def gelu(v):
    return 0.5 * v * (1.0 + np.tanh(np.sqrt(2.0 / np.pi) * (v + 0.044715 * v**3)))


K, K2, H, N, T, S, TB, P = 1024, 1536, 512, 768, 4096, 1024, 2048, 512


def setup_inputs():
    n = np.random.standard_normal
    s = mx_kscale(K)[:, None]
    s2 = mx_kscale(K2)[:, None]
    u = mx_kscale(H)[:, None]
    d = {}
    d["tab_words"], d["tab_scales"] = pack_weight(n((K, T)) * s, "e4m3")
    d["tab2_words"], d["tab2_scales"] = pack_weight(n((K2, TB)) * s2, "e4m3")
    d["offs"] = striped(np.random.permutation(T)[:S])
    d["offs2"] = striped(np.random.permutation(TB)[:P])
    d["pos1"] = striped(np.random.permutation(S)[:P])
    d["w1"] = (1.6 * n((K, H)) / K ** 0.5 / s * u.T).astype(np.float32)
    d["w2_words"], d["w2_scales"] = pack_weight(1.5 * n((K, H)) / K ** 0.5 / s, "e2m1")
    d["w3"] = (1.5 * n((K2, H)) / K2 ** 0.5 / s2).astype(np.float32)
    d["gain"] = (np.exp(0.4 * n(H)) * u[:, 0]).astype(np.float32)
    d["wgs"] = np.exp(0.3 * n((128, P))).astype(np.float32)
    d["w4_words"], d["w4_scales"] = pack_weight(1.2 * n((H, N)) / H ** 0.5 / u, "e4m3")
    d["base"] = (0.7 * n(N)).astype(np.float32)
    return d


def reference(tab_words, tab_scales, tab2_words, tab2_scales, offs, offs2, pos1, w1, w2_words, w2_scales, w3, gain, wgs, w4_words, w4_scales, base):
    v = unpack_weight(tab_words, tab_scales, "e4m3")[:, unstriped(offs)]
    v2 = unpack_weight(tab2_words, tab2_scales, "e4m3")[:, unstriped(offs2)]
    flow = mxq(f64(w1), 0, "e4m3").T @ v
    damp = unpack_weight(w2_words, w2_scales, "e2m1").T @ v
    a = flow / (1.0 + np.abs(damp))
    b = np.tanh(mxq(f64(w3), 0, "e4m3").T @ v2) * f64(gain)[:, None]
    placed = np.zeros((H, S))
    placed[:, unstriped(pos1)] = np.tile(f64(wgs), (H // 128, 1)) * b
    z = a + placed
    y = unpack_weight(w4_words, w4_scales, "e4m3").T @ mxq(z, 0, "e4m3")
    return y - f64(base)[:, None]

@@ -1,0 +1,314 @@
+from contextlib import ExitStack
+
+import concourse.mybir as mybir
+from concourse.masks import make_identity
+
+K, K2, H, N, T, S, TB, PL = 1024, 1536, 512, 768, 4096, 1024, 2048, 512
+FLOPS = 2 * (2 * K * H * S + K2 * H * PL + H * N * S)
+
+F32 = mybir.dt.float32
+BF16 = mybir.dt.bfloat16
+I32 = mybir.dt.int32
+U32 = mybir.dt.uint32
+U16 = mybir.dt.uint16
+U8 = mybir.dt.uint8
+FP8X4 = mybir.dt.float8_e4m3fn_x4
+FP4X4 = mybir.dt.float4_e2m1fn_x4
+ALU = mybir.AluOpType
+ACT = mybir.ActivationFunctionType
+
+P = 128
+PASS = 512
+A_PASSES = K // PASS
+B_PASSES = K2 // PASS
+ROW_TILES = H // P
+BLOCKS = S // P
+OUT_TILES = N // P
+HALF = S // 2
+GROUPS = (2, 2, 2, 1, 1)
+
+
+def tile_list_sap_flow_scores_kernel(
+    tc, tab_words, tab_scales, tab2_words, tab2_scales, offs, offs2, pos1, w1, w2_words, w2_scales, w3, gain, wgs,
+    w4_words, w4_scales, base, out
+):
+    nc = tc.nc
+    with ExitStack() as ctx:
+        keep = ctx.enter_context(tc.tile_pool(name="keep", bufs=1))
+        psum = ctx.enter_context(tc.psum_pool(name="psum", bufs=1))
+
+        def sb(name, shape, dtype, tag=None, bufs=1):
+            return keep.tile(shape, dtype, name=name, tag=tag or name, bufs=bufs, align_bytes=64)
+
+        def bank(name, tag, bufs):
+            return psum.tile([P, PASS], F32, name=name, tag=tag, bufs=bufs)
+
+        def words_of(dram, a):
+            return dram[a].rearrange("p t i -> p (t i)").bitcast(I32)
+
+        def rows_of(w, a):
+            return w[a * PASS : (a + 1) * PASS, :].rearrange("(p i) c -> p i c", i=4)
+
+        idx = keep.tile([P, S // 16], U16, name="idx")
+        idx2 = keep.tile([P, PL // 16], U16, name="idx2")
+        place = keep.tile([P, PL // 16], U16, name="place")
+        w3_raw = [[sb(f"w3_raw{s}_{a}", [P, 4, H // 2], F32) for a in range(B_PASSES)] for s in range(2)]
+        w1_raw = [sb(f"w1_raw{a}", [P, 4, H], F32) for a in range(A_PASSES)]
+        tab2 = [sb(f"tab2_{a}", [P, TB], I32) for a in range(B_PASSES)]
+        tab = [sb(f"tab_{a}", [P, T], I32) for a in range(A_PASSES)]
+        wgs_sb = sb("wgs_sb", [P, PL], F32)
+        w2_codes = sb("w2_codes", [P, A_PASSES, H // 2], I32)
+        w4_codes = sb("w4_codes", [P, N], I32)
+        tab2_sc = sb("tab2_sc", [P, TB // 4], I32)
+        tab_sc = sb("tab_sc", [P, T // 4], I32)
+        w2_sc = sb("w2_sc", [P, A_PASSES, H // 4], I32)
+        w4_sc = sb("w4_sc", [P, N // 4], I32)
+        v_sc = [sb(f"v_sc{a}", [P, S // 4], I32) for a in range(A_PASSES)]
+        for plane in (tab_sc, tab2_sc, w2_sc, w4_sc, *v_sc):
+            nc.vector.memset(plane[:], 0)
+
+        def load_w3(s, a):
+            nc.sync.dma_start(w3_raw[s][a][:], rows_of(w3, a)[:, :, s * (H // 2) : (s + 1) * (H // 2)])
+
+        def load_tab(a, h):
+            cols = slice(h * (T // 2), (h + 1) * (T // 2))
+            nc.sync.dma_start(tab[a][:, cols], words_of(tab_words, a)[:, cols])
+
+        nc.sync.dma_start(tab2[0][:], words_of(tab2_words, 0))
+        nc.sync.dma_start(tab_sc[0:P:4, :], tab_scales.rearrange("a q t -> (a q) t").bitcast(I32))
+        nc.sync.dma_start(idx[:], offs)
+        nc.sync.dma_start(idx2[:], offs2)
+        load_w3(0, 0)
+        nc.sync.dma_start(tab2[1][:], words_of(tab2_words, 1))
+        for q in range(4):
+            nc.sync.dma_start(tab2_sc[32 * q : 32 * q + 4 * B_PASSES, :], tab2_scales.bitcast(I32)[:, 4 * q : 4 * q + 4, :])
+        load_w3(0, 1)
+        load_w3(0, 2)
+        nc.sync.dma_start(tab2[2][:], words_of(tab2_words, 2))
+        nc.sync.dma_start(place[:], pos1)
+        nc.sync.dma_start(wgs_sb[:], wgs)
+        picked_sc = sb("picked_sc", [P, S], U8)
+        nc.vector.tensor_copy(picked_sc[:], tab_sc[:].bitcast(U8).indirect(idx[:]))
+
+        def move_scale_rows(a):
+            for q in range(4):
+                first = 64 * a + 16 * q
+                nc.sync.dma_start(v_sc[a][32 * q : 32 * q + 4, :], picked_sc[first : first + 16 : 4, :].bitcast(I32))
+
+        load_tab(0, 0)
+        for a in range(B_PASSES):
+            load_w3(1, a)
+        move_scale_rows(0)
+        load_tab(0, 1)
+        move_scale_rows(1)
+        load_tab(1, 0)
+        for q in range(4):
+            nc.sync.dma_start(
+                w2_sc[32 * q : 32 * q + 4, :, :], w2_scales.bitcast(I32)[:, 4 * q : 4 * q + 4, :].rearrange("a r w -> r a w")
+            )
+        nc.sync.dma_start(w2_codes[:], w2_words.bitcast(I32).rearrange("a p w -> p a w"))
+        load_tab(1, 1)
+        nc.sync.dma_start(w1_raw[0][:], rows_of(w1, 0))
+        for q in range(4):
+            nc.sync.dma_start(w4_sc[32 * q : 32 * q + 4, :], w4_scales.bitcast(I32)[0, 4 * q : 4 * q + 4, :])
+        nc.sync.dma_start(w1_raw[1][:], rows_of(w1, 1))
+        nc.sync.dma_start(w4_codes[:], words_of(w4_words, 0))
+
+        gain_sb = sb("gain_sb", [P, ROW_TILES], F32)
+        base_sb = sb("base_sb", [P, OUT_TILES], F32)
+        with nc.allow_non_contiguous_dma(reason="one value a partition and tile"):
+            nc.scalar.dma_start(gain_sb[:], gain.rearrange("(t p) -> p t", p=P))
+            nc.scalar.dma_start(base_sb[:], base.rearrange("(c p) -> p c", p=P))
+
+        pages = [sb(f"page{t}", [P, S], F32) for t in range(ROW_TILES)]
+        for t in range(ROW_TILES):
+            nc.gpsimd.memset(pages[t][:], 0.0)
+        ident = sb("ident", [P, P], F32)
+        make_identity(nc, ident[:])
+
+        def gather(dst, table, offsets, dtype):
+            nc.vector.tensor_copy(dst, table[:].bitcast(dtype).indirect(offsets))
+
+        def interleave(copy, raw, name):
+            grouped = sb(name, [P, raw.shape[2], 4], BF16, tag="grouped", bufs=3)
+            copy(grouped[:].rearrange("p (c n) i -> p c i n", n=4), raw[:].rearrange("p i (c n) -> p c i n", n=4))
+            return grouped
+
+        def quantize(src, name, width):
+            codes = sb(name + "_codes", [P, width], U32)
+            scales = sb(name + "_scales", [P, width], U8)
+            nc.vector.quantize_mx(out=codes[:].bitcast(FP8X4), scales=scales[:], in_=src)
+            return codes, scales
+
+        v2_sc = sb("v2_sc", [P, PL], U8)
+        gather(v2_sc[:], tab2_sc, idx2[:], U8)
+        early_weight = sb("early_weight", [P, 2, PL], F32)
+        v2 = [sb(f"v2_{a}", [P, PL], U32) for a in range(B_PASSES)]
+        response = []
+        for s in range(2):
+            b_banks = [bank(f"b_bank{s}_{i}", ("flow", "score")[s], 2) for i in range(2)]
+            for a in range(B_PASSES):
+                grouped = interleave(nc.scalar.copy, w3_raw[s][a], f"w3_grouped{s}_{a}")
+                if s == 0:
+                    gather(v2[a][:], tab2[a], idx2[:], U32)
+                codes, scales = quantize(grouped[:].rearrange("p c i -> p (c i)"), f"w3_{s}_{a}", H // 2)
+                for i in range(2):
+                    cols = slice(i * P, (i + 1) * P)
+                    nc.tensor.matmul_mx(
+                        b_banks[i][:], lhsT=codes[:, cols].bitcast(FP8X4), lhsT_scale=scales[:, cols],
+                        rhs=v2[a][:].bitcast(FP8X4), rhs_scale=v2_sc[4 * a : P, :], start=(a == 0), stop=(a == B_PASSES - 1),
+                    )
+            for i in range(2):
+                if s == 0:
+                    nc.scalar.activation(early_weight[:, i, :], wgs_sb[:], ACT.Copy, scale=gain_sb[:, i : i + 1])
+                r = sb(f"response{s}_{i}", [P, PL], F32)
+                nc.scalar.activation(r[:], b_banks[i][:], ACT.Tanh)
+                response.append(r)
+        warm = sb("warm", [P, 1], F32)
+        nc.scalar.activation(warm[:], response[3][:, 0:1], ACT.Abs_reciprocal_sqrt, bias=1.0, scale=0.5)
+
+        neg_base = sb("neg_base", [P, OUT_TILES], F32)
+        nc.vector.tensor_scalar(neg_base[:], base_sb[:], -1.0, None, ALU.mult)
+
+        def scatter(t, weight):
+            nc.vector.tensor_tensor(pages[t][:].indirect(place[:]), response[t][:], weight, ALU.mult)
+
+        for t in range(2):
+            scatter(t, early_weight[:, t, :])
+
+        v = [[None, None], [None, None]]
+        for a in range(A_PASSES):
+            for h in range(2):
+                v[a][h] = sb(f"v_{a}_{h}", [P, HALF], U32)
+                gather(v[a][h][:], tab[a], idx[:, h * (HALF // 16) : (h + 1) * (HALF // 16)], U32)
+
+        def late_weight(t, tag):
+            weight = sb(f"late_weight{t}", [P, PL], F32, tag=tag)
+            nc.vector.tensor_scalar(weight[:], wgs_sb[:], gain_sb[:, t : t + 1], None, ALU.mult)
+            return weight
+
+        scatter(2, late_weight(2, "tab_1")[:])
+        w1_q = []
+        for a in range(A_PASSES):
+            grouped = interleave(nc.vector.tensor_copy, w1_raw[a], f"w1_grouped{a}")
+            if a == A_PASSES - 1:
+                last_weight = late_weight(3, f"w1_raw{a}")
+            w1_q.append(quantize(grouped[:].rearrange("p c i -> p (c i)"), f"w1_{a}", H))
+        scatter(3, last_weight[:])
+
+        def product(dst, j, rhs_of):
+            h, c0 = divmod(j * P, HALF)
+            for a in range(A_PASSES):
+                rhs, rhs_scale = rhs_of(a)
+                nc.tensor.matmul_mx(
+                    dst[:], lhsT=v[a][h][:, c0 : c0 + P].bitcast(FP8X4), lhsT_scale=v_sc[a][:].bitcast(U8)[:, j * P : (j + 1) * P],
+                    rhs=rhs, rhs_scale=rhs_scale, start=(a == 0), stop=(a == A_PASSES - 1),
+                )
+
+        damped = {}
+        z_groups = {}
+        z_q = []
+        group_of = {}
+        j0 = 0
+        for g, n_blocks in enumerate(GROUPS):
+            for i in range(n_blocks):
+                group_of[j0 + i] = (g, j0, n_blocks)
+            j0 = j0 + n_blocks
+
+        damp_banks = (("flow", 2), ("flow", 2), ("placed", 2), ("placed", 2), ("score", 2), ("score", 2), ("turned", 2), ("turned", 2))
+        inverse = sb("inverse", [P, BLOCKS, H], F32)
+
+        def damp_size(j):
+            d = bank(f"damp{j}", *damp_banks[j])
+            product(d, j, lambda a: (w2_codes[:, a, :].bitcast(U8).bitcast(FP4X4), w2_sc[:, a, :].bitcast(U8)))
+            nc.scalar.activation(inverse[:, j, :], d[:], ACT.Abs)
+
+        def damp_square(j0, j1):
+            nc.scalar.activation(inverse[:, j0:j1, :], inverse[:, j0:j1, :], ACT.Square, bias=1.0)
+
+        def damp_inverse(j0, j1):
+            nc.scalar.activation(inverse[:, j0:j1, :], inverse[:, j0:j1, :], ACT.Abs_reciprocal_sqrt)
+
+        for j in range(4):
+            damp_size(j)
+        damp_square(0, 4)
+        damp_size(4)
+        damp_size(5)
+        damp_inverse(0, 4)
+        damp_size(6)
+        damp_size(7)
+        damp_square(4, 6)
+        damp_square(6, 8)
+        damp_inverse(4, 6)
+        damp_inverse(6, 8)
+
+        def flow(j):
+            f = bank(f"flow{j}", "score" if j in (2, 3) else "flow", 2)
+            product(f, j, lambda a: (w1_q[a][0][:].bitcast(FP8X4), w1_q[a][1][:]))
+            damped[j] = sb(f"damped{j}", [P, H], F32, tag="damped", bufs=3)
+            nc.vector.tensor_tensor(damped[j][:], f[:], inverse[:, j, :], ALU.mult)
+
+        def join(j):
+            placed = bank(f"placed{j}", "placed", 2)
+            for t in range(ROW_TILES):
+                nc.tensor.transpose(placed[:, t * P : (t + 1) * P], pages[t][:, j * P : (j + 1) * P], ident[:])
+            z_rows = sb(f"z_rows{j}", [P, H], BF16, tag="z_rows", bufs=3)
+            nc.vector.tensor_tensor(
+                z_rows[:].rearrange("j (u p e) -> j u p e", u=2, e=2),
+                placed[:].rearrange("j (p u e) -> j u p e", u=2, e=2),
+                damped[j][:].rearrange("j (p u e) -> j u p e", u=2, e=2),
+                ALU.add,
+            )
+            turned = bank(f"turned{j}", "turned", 2)
+            pairs = z_rows[:].bitcast(F32)
+            for u in range(2):
+                nc.tensor.transpose(turned[:, u * P : (u + 1) * P], pairs[:, u * P : (u + 1) * P], ident[:])
+            g, first, n_blocks = group_of[j]
+            if j == first:
+                z_groups[g] = sb(f"z_group{g}", [P, n_blocks * PASS], BF16)
+            i = j - first
+            nc.scalar.copy(
+                z_groups[g][:, i * PASS : (i + 1) * PASS].bitcast(F32).rearrange("p (j u) -> p j u", u=2),
+                turned[:, 0 : 2 * P].rearrange("p (u j) -> p j u", u=2),
+            )
+            if i == n_blocks - 1:
+                z_q.append((g, first, n_blocks, *quantize(z_groups[g][:], f"z_{g}", n_blocks * P)))
+
+        def scores(g, first, n_blocks, codes, scales):
+            width = n_blocks * P
+            per_bank = min(PASS // width, OUT_TILES // 2)
+            for n, c0 in enumerate(range(0, OUT_TILES, per_bank)):
+                acc = bank(f"score{g}_{c0}", "score", 2)
+                for i in range(per_bank):
+                    cols = slice((c0 + i) * P, (c0 + i + 1) * P)
+                    nc.tensor.matmul_mx(
+                        acc[:, i * width : (i + 1) * width], lhsT=w4_codes[:, cols].bitcast(FP8X4),
+                        lhsT_scale=w4_sc[:].bitcast(U8)[:, cols], rhs=codes[:].bitcast(FP8X4), rhs_scale=scales[:],
+                        start=True, stop=True,
+                    )
+                staged = sb(f"staged{g}_{c0}", [P, per_bank, width], F32, tag="staged", bufs=6)
+                if n_blocks == 1:
+                    nc.vector.tensor_tensor(
+                        staged[:], acc[:, 0 : per_bank * width].rearrange("p (c j) -> p c j", j=width),
+                        base_sb[:, c0 : c0 + per_bank].unsqueeze(2).to_broadcast([P, per_bank, width]), ALU.subtract,
+                    )
+                else:
+                    for i in range(per_bank):
+                        nc.scalar.activation(
+                            staged[:, i, :], acc[:, i * width : (i + 1) * width], ACT.Identity,
+                            bias=neg_base[:, c0 + i : c0 + i + 1],
+                        )
+                nc.sync.dma_start(
+                    out[c0 * P : (c0 + per_bank) * P, first * P : first * P + width].rearrange("(c p) j -> p c j", p=P),
+                    staged[:],
+                )
+
+        flow(0)
+        for j in range(BLOCKS):
+            if j + 1 < BLOCKS:
+                flow(j + 1)
+            join(j)
+            if j in (2, 4):
+                scores(*z_q[j // 2 - 1])
+        for group in z_q[2:]:
+            scores(*group)

@@ -64,7 +64,10 @@ def tile_list_sap_flow_scores_kernel(
         w2_sc = sb("w2_sc", [P, A_PASSES, H // 4], I32)
         w4_sc = sb("w4_sc", [P, N // 4], I32)
         v_sc = [sb(f"v_sc{a}", [P, S // 4], I32) for a in range(A_PASSES)]
-        for plane in (tab_sc, tab2_sc, w2_sc, w4_sc, *v_sc):
+        vectors = sb("vectors", [P, P], F32)
+        nc.gpsimd.memset(tab2_sc[:], 0)
+        nc.gpsimd.memset(vectors[:], 0.0)
+        for plane in (tab_sc, w2_sc, w4_sc, *v_sc):
             nc.vector.memset(plane[:], 0)
 
         def load_w3(s, a):
@@ -83,6 +86,8 @@ def tile_list_sap_flow_scores_kernel(
         for q in range(4):
             nc.sync.dma_start(tab2_sc[32 * q : 32 * q + 4 * B_PASSES, :], tab2_scales.bitcast(I32)[:, 4 * q : 4 * q + 4, :])
         load_w3(0, 1)
+        nc.sync.dma_start(vectors[0:ROW_TILES, :], gain.rearrange("(t p) -> t p", p=P))
+        nc.sync.dma_start(vectors[32 : 32 + OUT_TILES, :], base.rearrange("(c p) -> c p", p=P))
         load_w3(0, 2)
         nc.sync.dma_start(tab2[2][:], words_of(tab2_words, 2))
         nc.sync.dma_start(place[:], pos1)
@@ -108,23 +113,24 @@ def tile_list_sap_flow_scores_kernel(
             )
         nc.sync.dma_start(w2_codes[:], w2_words.bitcast(I32).rearrange("a p w -> p a w"))
         load_tab(1, 1)
-        nc.sync.dma_start(w1_raw[0][:], rows_of(w1, 0))
+        for a in range(A_PASSES):
+            nc.sync.dma_start(w1_raw[a][:], rows_of(w1, a))
+        nc.sync.dma_start(w4_codes[:], words_of(w4_words, 0))
         for q in range(4):
             nc.sync.dma_start(w4_sc[32 * q : 32 * q + 4, :], w4_scales.bitcast(I32)[0, 4 * q : 4 * q + 4, :])
-        nc.sync.dma_start(w1_raw[1][:], rows_of(w1, 1))
-        nc.sync.dma_start(w4_codes[:], words_of(w4_words, 0))
 
-        gain_sb = sb("gain_sb", [P, ROW_TILES], F32)
-        base_sb = sb("base_sb", [P, OUT_TILES], F32)
-        with nc.allow_non_contiguous_dma(reason="one value a partition and tile"):
-            nc.scalar.dma_start(gain_sb[:], gain.rearrange("(t p) -> p t", p=P))
-            nc.scalar.dma_start(base_sb[:], base.rearrange("(c p) -> p c", p=P))
-
+        ident = sb("ident", [P, P], F32)
+        make_identity(nc, ident[:])
         pages = [sb(f"page{t}", [P, S], F32) for t in range(ROW_TILES)]
         for t in range(ROW_TILES):
             nc.gpsimd.memset(pages[t][:], 0.0)
-        ident = sb("ident", [P, P], F32)
-        make_identity(nc, ident[:])
+
+        vectors_turned = bank("vectors_turned", "turned", 2)
+        nc.tensor.transpose(vectors_turned[:, 0:P], vectors[:], ident[:])
+        gain_sb = sb("gain_sb", [P, ROW_TILES], F32)
+        neg_base = sb("neg_base", [P, OUT_TILES], F32)
+        nc.scalar.activation(gain_sb[:], vectors_turned[:, 0:ROW_TILES], ACT.Copy)
+        nc.scalar.activation(neg_base[:], vectors_turned[:, 32 : 32 + OUT_TILES], ACT.Copy, scale=-1.0)
 
         def gather(dst, table, offsets, dtype):
             nc.vector.tensor_copy(dst, table[:].bitcast(dtype).indirect(offsets))
@@ -167,9 +173,6 @@ def tile_list_sap_flow_scores_kernel(
         warm = sb("warm", [P, 1], F32)
         nc.scalar.activation(warm[:], response[3][:, 0:1], ACT.Abs_reciprocal_sqrt, bias=1.0, scale=0.5)
 
-        neg_base = sb("neg_base", [P, OUT_TILES], F32)
-        nc.vector.tensor_scalar(neg_base[:], base_sb[:], -1.0, None, ALU.mult)
-
         def scatter(t, weight):
             nc.vector.tensor_tensor(pages[t][:].indirect(place[:]), response[t][:], weight, ALU.mult)
 
@@ -196,6 +199,12 @@ def tile_list_sap_flow_scores_kernel(
             w1_q.append(quantize(grouped[:].rearrange("p c i -> p (c i)"), f"w1_{a}", H))
         scatter(3, last_weight[:])
 
+        def by_pairs(natural):
+            return natural.rearrange("j (p u e) -> j u p e", u=2, e=2)
+
+        def paired(reordered):
+            return reordered.rearrange("j (u p e) -> j u p e", u=2, e=2)
+
         def product(dst, j, rhs_of):
             h, c0 = divmod(j * P, HALF)
             for a in range(A_PASSES):
@@ -221,7 +230,7 @@ def tile_list_sap_flow_scores_kernel(
         def damp_size(j):
             d = bank(f"damp{j}", *damp_banks[j])
             product(d, j, lambda a: (w2_codes[:, a, :].bitcast(U8).bitcast(FP4X4), w2_sc[:, a, :].bitcast(U8)))
-            nc.scalar.activation(inverse[:, j, :], d[:], ACT.Abs)
+            nc.scalar.activation(paired(inverse[:, j, :]), by_pairs(d[:]), ACT.Abs)
 
         def damp_square(j0, j1):
             nc.scalar.activation(inverse[:, j0:j1, :], inverse[:, j0:j1, :], ACT.Square, bias=1.0)
@@ -246,19 +255,14 @@ def tile_list_sap_flow_scores_kernel(
             f = bank(f"flow{j}", "score" if j in (2, 3) else "flow", 2)
             product(f, j, lambda a: (w1_q[a][0][:].bitcast(FP8X4), w1_q[a][1][:]))
             damped[j] = sb(f"damped{j}", [P, H], F32, tag="damped", bufs=3)
-            nc.vector.tensor_tensor(damped[j][:], f[:], inverse[:, j, :], ALU.mult)
+            nc.vector.tensor_tensor(paired(damped[j][:]), by_pairs(f[:]), paired(inverse[:, j, :]), ALU.mult)
 
         def join(j):
             placed = bank(f"placed{j}", "placed", 2)
             for t in range(ROW_TILES):
                 nc.tensor.transpose(placed[:, t * P : (t + 1) * P], pages[t][:, j * P : (j + 1) * P], ident[:])
             z_rows = sb(f"z_rows{j}", [P, H], BF16, tag="z_rows", bufs=3)
-            nc.vector.tensor_tensor(
-                z_rows[:].rearrange("j (u p e) -> j u p e", u=2, e=2),
-                placed[:].rearrange("j (p u e) -> j u p e", u=2, e=2),
-                damped[j][:].rearrange("j (p u e) -> j u p e", u=2, e=2),
-                ALU.add,
-            )
+            nc.vector.tensor_tensor(paired(z_rows[:]), by_pairs(placed[:]), paired(damped[j][:]), ALU.add)
             turned = bank(f"turned{j}", "turned", 2)
             pairs = z_rows[:].bitcast(F32)
             for u in range(2):
@@ -278,7 +282,7 @@ def tile_list_sap_flow_scores_kernel(
             width = n_blocks * P
             per_bank = min(PASS // width, OUT_TILES // 2)
             for n, c0 in enumerate(range(0, OUT_TILES, per_bank)):
-                acc = bank(f"score{g}_{c0}", "score", 2)
+                acc = bank(f"score{g}_{c0}", ("score", "score", "score", "flow", "placed")[g], 2)
                 for i in range(per_bank):
                     cols = slice((c0 + i) * P, (c0 + i + 1) * P)
                     nc.tensor.matmul_mx(
@@ -290,7 +294,7 @@ def tile_list_sap_flow_scores_kernel(
                 if n_blocks == 1:
                     nc.vector.tensor_tensor(
                         staged[:], acc[:, 0 : per_bank * width].rearrange("p (c j) -> p c j", j=width),
-                        base_sb[:, c0 : c0 + per_bank].unsqueeze(2).to_broadcast([P, per_bank, width]), ALU.subtract,
+                        neg_base[:, c0 : c0 + per_bank].unsqueeze(2).to_broadcast([P, per_bank, width]), ALU.add,
                     )
                 else:
                     for i in range(per_bank):

from contextlib import ExitStack

import concourse.mybir as mybir
from concourse.masks import make_identity

K, K2, H, N, T, S, TB, PL = 1024, 1536, 512, 768, 4096, 1024, 2048, 512
FLOPS = 2 * (2 * K * H * S + K2 * H * PL + H * N * S)

F32 = mybir.dt.float32
BF16 = mybir.dt.bfloat16
I32 = mybir.dt.int32
U32 = mybir.dt.uint32
U16 = mybir.dt.uint16
U8 = mybir.dt.uint8
FP8X4 = mybir.dt.float8_e4m3fn_x4
FP4X4 = mybir.dt.float4_e2m1fn_x4
ALU = mybir.AluOpType
ACT = mybir.ActivationFunctionType

P = 128
PASS = 512
A_PASSES = K // PASS
B_PASSES = K2 // PASS
ROW_TILES = H // P
BLOCKS = S // P
OUT_TILES = N // P
HALF = S // 2
GROUPS = (2, 2, 2, 1, 1)


def tile_list_sap_flow_scores_kernel(
    tc, tab_words, tab_scales, tab2_words, tab2_scales, offs, offs2, pos1, w1, w2_words, w2_scales, w3, gain, wgs,
    w4_words, w4_scales, base, out
):
    nc = tc.nc
    with ExitStack() as ctx:
        keep = ctx.enter_context(tc.tile_pool(name="keep", bufs=1))
        psum = ctx.enter_context(tc.psum_pool(name="psum", bufs=1))

        def sb(name, shape, dtype, tag=None, bufs=1):
            return keep.tile(shape, dtype, name=name, tag=tag or name, bufs=bufs, align_bytes=64)

        def bank(name, tag, bufs):
            return psum.tile([P, PASS], F32, name=name, tag=tag, bufs=bufs)

        def words_of(dram, a):
            return dram[a].rearrange("p t i -> p (t i)").bitcast(I32)

        def rows_of(w, a):
            return w[a * PASS : (a + 1) * PASS, :].rearrange("(p i) c -> p i c", i=4)

        idx = keep.tile([P, S // 16], U16, name="idx")
        idx2 = keep.tile([P, PL // 16], U16, name="idx2")
        place = keep.tile([P, PL // 16], U16, name="place")
        w3_raw = [[sb(f"w3_raw{s}_{a}", [P, 4, H // 2], F32) for a in range(B_PASSES)] for s in range(2)]
        w1_raw = [sb(f"w1_raw{a}", [P, 4, H], F32) for a in range(A_PASSES)]
        tab2 = [sb(f"tab2_{a}", [P, TB], I32) for a in range(B_PASSES)]
        tab = [sb(f"tab_{a}", [P, T], I32) for a in range(A_PASSES)]
        wgs_sb = sb("wgs_sb", [P, PL], F32)
        w2_codes = sb("w2_codes", [P, A_PASSES, H // 2], I32)
        w4_codes = sb("w4_codes", [P, N], I32)
        tab2_sc = sb("tab2_sc", [P, TB // 4], I32)
        tab_sc = sb("tab_sc", [P, T // 4], I32)
        w2_sc = sb("w2_sc", [P, A_PASSES, H // 4], I32)
        w4_sc = sb("w4_sc", [P, N // 4], I32)
        v_sc = [sb(f"v_sc{a}", [P, S // 4], I32) for a in range(A_PASSES)]
        vectors = sb("vectors", [P, P], F32)
        nc.gpsimd.memset(tab2_sc[:], 0)
        nc.gpsimd.memset(vectors[:], 0.0)
        for plane in (tab_sc, w2_sc, w4_sc, *v_sc):
            nc.vector.memset(plane[:], 0)

        def load_w3(s, a):
            nc.sync.dma_start(w3_raw[s][a][:], rows_of(w3, a)[:, :, s * (H // 2) : (s + 1) * (H // 2)])

        def load_tab(a, h):
            cols = slice(h * (T // 2), (h + 1) * (T // 2))
            nc.sync.dma_start(tab[a][:, cols], words_of(tab_words, a)[:, cols])

        nc.sync.dma_start(tab2[0][:], words_of(tab2_words, 0))
        nc.sync.dma_start(tab_sc[0:P:4, :], tab_scales.rearrange("a q t -> (a q) t").bitcast(I32))
        nc.sync.dma_start(idx[:], offs)
        nc.sync.dma_start(idx2[:], offs2)
        load_w3(0, 0)
        nc.sync.dma_start(tab2[1][:], words_of(tab2_words, 1))
        for q in range(4):
            nc.sync.dma_start(tab2_sc[32 * q : 32 * q + 4 * B_PASSES, :], tab2_scales.bitcast(I32)[:, 4 * q : 4 * q + 4, :])
        load_w3(0, 1)
        nc.sync.dma_start(vectors[0:ROW_TILES, :], gain.rearrange("(t p) -> t p", p=P))
        nc.sync.dma_start(vectors[32 : 32 + OUT_TILES, :], base.rearrange("(c p) -> c p", p=P))
        load_w3(0, 2)
        nc.sync.dma_start(tab2[2][:], words_of(tab2_words, 2))
        nc.sync.dma_start(place[:], pos1)
        nc.sync.dma_start(wgs_sb[:], wgs)
        picked_sc = sb("picked_sc", [P, S], U8)
        nc.vector.tensor_copy(picked_sc[:], tab_sc[:].bitcast(U8).indirect(idx[:]))

        def move_scale_rows(a):
            for q in range(4):
                first = 64 * a + 16 * q
                nc.sync.dma_start(v_sc[a][32 * q : 32 * q + 4, :], picked_sc[first : first + 16 : 4, :].bitcast(I32))

        load_tab(0, 0)
        for a in range(B_PASSES):
            load_w3(1, a)
        move_scale_rows(0)
        load_tab(0, 1)
        move_scale_rows(1)
        load_tab(1, 0)
        for q in range(4):
            nc.sync.dma_start(
                w2_sc[32 * q : 32 * q + 4, :, :], w2_scales.bitcast(I32)[:, 4 * q : 4 * q + 4, :].rearrange("a r w -> r a w")
            )
        nc.sync.dma_start(w2_codes[:], w2_words.bitcast(I32).rearrange("a p w -> p a w"))
        load_tab(1, 1)
        for a in range(A_PASSES):
            nc.sync.dma_start(w1_raw[a][:], rows_of(w1, a))
        nc.sync.dma_start(w4_codes[:], words_of(w4_words, 0))
        for q in range(4):
            nc.sync.dma_start(w4_sc[32 * q : 32 * q + 4, :], w4_scales.bitcast(I32)[0, 4 * q : 4 * q + 4, :])

        ident = sb("ident", [P, P], F32)
        make_identity(nc, ident[:])
        pages = [sb(f"page{t}", [P, S], F32) for t in range(ROW_TILES)]
        for t in range(ROW_TILES):
            nc.gpsimd.memset(pages[t][:], 0.0)

        vectors_turned = bank("vectors_turned", "turned", 2)
        nc.tensor.transpose(vectors_turned[:, 0:P], vectors[:], ident[:])
        gain_sb = sb("gain_sb", [P, ROW_TILES], F32)
        neg_base = sb("neg_base", [P, OUT_TILES], F32)
        nc.scalar.activation(gain_sb[:], vectors_turned[:, 0:ROW_TILES], ACT.Copy)
        nc.scalar.activation(neg_base[:], vectors_turned[:, 32 : 32 + OUT_TILES], ACT.Copy, scale=-1.0)

        def gather(dst, table, offsets, dtype):
            nc.vector.tensor_copy(dst, table[:].bitcast(dtype).indirect(offsets))

        def interleave(copy, raw, name):
            grouped = sb(name, [P, raw.shape[2], 4], BF16, tag="grouped", bufs=3)
            copy(grouped[:].rearrange("p (c n) i -> p c i n", n=4), raw[:].rearrange("p i (c n) -> p c i n", n=4))
            return grouped

        def quantize(src, name, width):
            codes = sb(name + "_codes", [P, width], U32)
            scales = sb(name + "_scales", [P, width], U8)
            nc.vector.quantize_mx(out=codes[:].bitcast(FP8X4), scales=scales[:], in_=src)
            return codes, scales

        v2_sc = sb("v2_sc", [P, PL], U8)
        gather(v2_sc[:], tab2_sc, idx2[:], U8)
        early_weight = sb("early_weight", [P, 2, PL], F32)
        v2 = [sb(f"v2_{a}", [P, PL], U32) for a in range(B_PASSES)]
        response = []
        for s in range(2):
            b_banks = [bank(f"b_bank{s}_{i}", ("flow", "score")[s], 2) for i in range(2)]
            for a in range(B_PASSES):
                grouped = interleave(nc.scalar.copy, w3_raw[s][a], f"w3_grouped{s}_{a}")
                if s == 0:
                    gather(v2[a][:], tab2[a], idx2[:], U32)
                codes, scales = quantize(grouped[:].rearrange("p c i -> p (c i)"), f"w3_{s}_{a}", H // 2)
                for i in range(2):
                    cols = slice(i * P, (i + 1) * P)
                    nc.tensor.matmul_mx(
                        b_banks[i][:], lhsT=codes[:, cols].bitcast(FP8X4), lhsT_scale=scales[:, cols],
                        rhs=v2[a][:].bitcast(FP8X4), rhs_scale=v2_sc[4 * a : P, :], start=(a == 0), stop=(a == B_PASSES - 1),
                    )
            for i in range(2):
                if s == 0:
                    nc.scalar.activation(early_weight[:, i, :], wgs_sb[:], ACT.Copy, scale=gain_sb[:, i : i + 1])
                r = sb(f"response{s}_{i}", [P, PL], F32)
                nc.scalar.activation(r[:], b_banks[i][:], ACT.Tanh)
                response.append(r)
        warm = sb("warm", [P, 1], F32)
        nc.scalar.activation(warm[:], response[3][:, 0:1], ACT.Abs_reciprocal_sqrt, bias=1.0, scale=0.5)

        def scatter(t, weight):
            nc.vector.tensor_tensor(pages[t][:].indirect(place[:]), response[t][:], weight, ALU.mult)

        for t in range(2):
            scatter(t, early_weight[:, t, :])

        v = [[None, None], [None, None]]
        for a in range(A_PASSES):
            for h in range(2):
                v[a][h] = sb(f"v_{a}_{h}", [P, HALF], U32)
                gather(v[a][h][:], tab[a], idx[:, h * (HALF // 16) : (h + 1) * (HALF // 16)], U32)

        def late_weight(t, tag):
            weight = sb(f"late_weight{t}", [P, PL], F32, tag=tag)
            nc.vector.tensor_scalar(weight[:], wgs_sb[:], gain_sb[:, t : t + 1], None, ALU.mult)
            return weight

        scatter(2, late_weight(2, "tab_1")[:])
        w1_q = []
        for a in range(A_PASSES):
            grouped = interleave(nc.vector.tensor_copy, w1_raw[a], f"w1_grouped{a}")
            if a == A_PASSES - 1:
                last_weight = late_weight(3, f"w1_raw{a}")
            w1_q.append(quantize(grouped[:].rearrange("p c i -> p (c i)"), f"w1_{a}", H))
        scatter(3, last_weight[:])

        def by_pairs(natural):
            return natural.rearrange("j (p u e) -> j u p e", u=2, e=2)

        def paired(reordered):
            return reordered.rearrange("j (u p e) -> j u p e", u=2, e=2)

        def product(dst, j, rhs_of):
            h, c0 = divmod(j * P, HALF)
            for a in range(A_PASSES):
                rhs, rhs_scale = rhs_of(a)
                nc.tensor.matmul_mx(
                    dst[:], lhsT=v[a][h][:, c0 : c0 + P].bitcast(FP8X4), lhsT_scale=v_sc[a][:].bitcast(U8)[:, j * P : (j + 1) * P],
                    rhs=rhs, rhs_scale=rhs_scale, start=(a == 0), stop=(a == A_PASSES - 1),
                )

        damped = {}
        z_groups = {}
        z_q = []
        group_of = {}
        j0 = 0
        for g, n_blocks in enumerate(GROUPS):
            for i in range(n_blocks):
                group_of[j0 + i] = (g, j0, n_blocks)
            j0 = j0 + n_blocks

        damp_banks = (("flow", 2), ("flow", 2), ("placed", 2), ("placed", 2), ("score", 2), ("score", 2), ("turned", 2), ("turned", 2))
        inverse = sb("inverse", [P, BLOCKS, H], F32)

        def damp_size(j):
            d = bank(f"damp{j}", *damp_banks[j])
            product(d, j, lambda a: (w2_codes[:, a, :].bitcast(U8).bitcast(FP4X4), w2_sc[:, a, :].bitcast(U8)))
            nc.scalar.activation(paired(inverse[:, j, :]), by_pairs(d[:]), ACT.Abs)

        def damp_square(j0, j1):
            nc.scalar.activation(inverse[:, j0:j1, :], inverse[:, j0:j1, :], ACT.Square, bias=1.0)

        def damp_inverse(j0, j1):
            nc.scalar.activation(inverse[:, j0:j1, :], inverse[:, j0:j1, :], ACT.Abs_reciprocal_sqrt)

        for j in range(4):
            damp_size(j)
        damp_square(0, 4)
        damp_size(4)
        damp_size(5)
        damp_inverse(0, 4)
        damp_size(6)
        damp_size(7)
        damp_square(4, 6)
        damp_square(6, 8)
        damp_inverse(4, 6)
        damp_inverse(6, 8)

        def flow(j):
            f = bank(f"flow{j}", "score" if j in (2, 3) else "flow", 2)
            product(f, j, lambda a: (w1_q[a][0][:].bitcast(FP8X4), w1_q[a][1][:]))
            damped[j] = sb(f"damped{j}", [P, H], F32, tag="damped", bufs=3)
            nc.vector.tensor_tensor(paired(damped[j][:]), by_pairs(f[:]), paired(inverse[:, j, :]), ALU.mult)

        def join(j):
            placed = bank(f"placed{j}", "placed", 2)
            for t in range(ROW_TILES):
                nc.tensor.transpose(placed[:, t * P : (t + 1) * P], pages[t][:, j * P : (j + 1) * P], ident[:])
            z_rows = sb(f"z_rows{j}", [P, H], BF16, tag="z_rows", bufs=3)
            nc.vector.tensor_tensor(paired(z_rows[:]), by_pairs(placed[:]), paired(damped[j][:]), ALU.add)
            turned = bank(f"turned{j}", "turned", 2)
            pairs = z_rows[:].bitcast(F32)
            for u in range(2):
                nc.tensor.transpose(turned[:, u * P : (u + 1) * P], pairs[:, u * P : (u + 1) * P], ident[:])
            g, first, n_blocks = group_of[j]
            if j == first:
                z_groups[g] = sb(f"z_group{g}", [P, n_blocks * PASS], BF16)
            i = j - first
            nc.scalar.copy(
                z_groups[g][:, i * PASS : (i + 1) * PASS].bitcast(F32).rearrange("p (j u) -> p j u", u=2),
                turned[:, 0 : 2 * P].rearrange("p (u j) -> p j u", u=2),
            )
            if i == n_blocks - 1:
                z_q.append((g, first, n_blocks, *quantize(z_groups[g][:], f"z_{g}", n_blocks * P)))

        def scores(g, first, n_blocks, codes, scales):
            width = n_blocks * P
            per_bank = min(PASS // width, OUT_TILES // 2)
            for n, c0 in enumerate(range(0, OUT_TILES, per_bank)):
                acc = bank(f"score{g}_{c0}", ("score", "score", "score", "flow", "placed")[g], 2)
                for i in range(per_bank):
                    cols = slice((c0 + i) * P, (c0 + i + 1) * P)
                    nc.tensor.matmul_mx(
                        acc[:, i * width : (i + 1) * width], lhsT=w4_codes[:, cols].bitcast(FP8X4),
                        lhsT_scale=w4_sc[:].bitcast(U8)[:, cols], rhs=codes[:].bitcast(FP8X4), rhs_scale=scales[:],
                        start=True, stop=True,
                    )
                staged = sb(f"staged{g}_{c0}", [P, per_bank, width], F32, tag="staged", bufs=6)
                if n_blocks == 1:
                    nc.vector.tensor_tensor(
                        staged[:], acc[:, 0 : per_bank * width].rearrange("p (c j) -> p c j", j=width),
                        neg_base[:, c0 : c0 + per_bank].unsqueeze(2).to_broadcast([P, per_bank, width]), ALU.add,
                    )
                else:
                    for i in range(per_bank):
                        nc.scalar.activation(
                            staged[:, i, :], acc[:, i * width : (i + 1) * width], ACT.Identity,
                            bias=neg_base[:, c0 + i : c0 + i + 1],
                        )
                nc.sync.dma_start(
                    out[c0 * P : (c0 + per_bank) * P, first * P : first * P + width].rearrange("(c p) j -> p c j", p=P),
                    staged[:],
                )

        flow(0)
        for j in range(BLOCKS):
            if j + 1 < BLOCKS:
                flow(j + 1)
            join(j)
            if j in (2, 4):
                scores(*z_q[j // 2 - 1])
        for group in z_q[2:]:
            scores(*group)
